import numpy as np
import ml_dtypes


def mxq(x, axis, fmt="e4m3"):
    dtype, down = {"e4m3": (ml_dtypes.float8_e4m3fn, 7), "e5m2": (ml_dtypes.float8_e5m2, 14)}[fmt]
    v = np.moveaxis(np.asarray(x, np.float32).astype(ml_dtypes.bfloat16).astype(np.float64), axis, -1)
    blocks = v.reshape(v.shape[:-1] + (-1, 32))
    amax = np.abs(blocks).max(-1, keepdims=True)
    byte = np.maximum(np.where(amax > 0, np.frexp(amax)[1] - 1 + 127, 0) - down, 1)
    scale = np.exp2(byte - 127.0)
    codes = (blocks / scale).astype(np.float32).astype(dtype).astype(np.float64)
    return np.moveaxis((codes * scale).reshape(v.shape), -1, axis)


WIDE = False


def mx_kscale(k):
    if not WIDE:
        return np.ones(k)
    levels = np.array([10, -10, 5, -5, 0])
    if k % 512:
        return np.exp2(np.random.permutation(np.resize(levels, k // 32))).repeat(32)
    a = np.empty((k // 512, 16))
    for p in range(k // 512):
        a[p, :8] = np.random.permutation(np.resize(levels, 8))
        for g in range(8):
            far = levels[np.abs(levels - a[p, g]) >= 10]
            a[p, g + 8] = far[np.random.randint(len(far))]
    return np.exp2(a.ravel()).repeat(32)


def f64(x):
    return np.asarray(x).astype(np.float64)


def striped(idx):
    return np.tile(idx.reshape(-1, 16).T, (8, 1)).astype(np.uint16)


def unstriped(offs):
    return offs[:16].T.reshape(-1).astype(np.int64)


def striped8(idx):
    return np.concatenate([x.reshape(-1, 16).T for x in idx]).astype(np.uint16)


def runs(offs, k):
    lists = np.stack([offs[16 * r : 16 * r + 16].T.reshape(-1) for r in range(8)]).astype(np.int64)
    return lists[np.arange(k) % 512 // 64]


def pack_weight(w):
    k, n = w.shape
    w = f64(np.asarray(w, np.float32).astype(ml_dtypes.bfloat16)).reshape(k // 32, 32, n)
    amax = np.abs(w).max(1)
    byte = np.clip(np.where(amax > 0, np.frexp(amax)[1] - 1 + 127 - 7, 1), 1, 254)
    scaled = (w * np.exp2(127.0 - byte)[:, None, :]).reshape(k, n).astype(np.float32)
    words = np.ascontiguousarray(scaled.reshape(k // 512, 128, 4, n).transpose(0, 1, 3, 2)).astype(ml_dtypes.float8_e4m3fn).view(np.uint8)
    return words, np.ascontiguousarray(byte.astype(np.uint8).reshape(k // 512, 16, n))


def unpack_weight(words, scales):
    g, p, n, _ = words.shape
    vals = np.ascontiguousarray(words).view(ml_dtypes.float8_e4m3fn).astype(np.float64) * np.repeat(np.exp2(scales.astype(np.float64) - 127.0), 8, axis=1)[..., None]
    return vals.transpose(0, 1, 3, 2).reshape(g * 512, n)


def sigmoid(v):
    return 1.0 / (1.0 + np.exp(-np.maximum(v, -700.0)))


K, T, S, V, H, W = 512, 2048, 512, 256, 512, 1024


def setup_inputs():
    n = np.random.standard_normal
    s = mx_kscale(K)[:, None]
    u = mx_kscale(S)
    packed_xT = pack_weight(n((K, T)) * s)
    return {
        "x_words": packed_xT[0],
        "x_scales": packed_xT[1],
        "w1": (n((K, H)) / np.sqrt(K) / s).astype(np.float32),
        "w2": (n((K, H)) / np.sqrt(K) / s).astype(np.float32),
        "sl": np.random.uniform(1.0, 2.0, (H, 1)).astype(np.float32),
        "th": (0.5 * n((H, 1))).astype(np.float32),
        "w3": (n((K, H)) / np.sqrt(K) / s).astype(np.float32),
        "tau": np.random.uniform(0.3, 0.9, (H, 1)).astype(np.float32),
        "tau2": np.random.uniform(0.3, 0.9, (H, 1)).astype(np.float32),
        "ga": (np.random.uniform(0.5, 1.5, (H, 1)) * u[:, None]).astype(np.float32),
        "gb": (np.random.uniform(0.5, 1.5, (H, 1)) / u[:, None]).astype(np.float32),
        "tau3": np.random.uniform(0.3, 0.9, (S, 1)).astype(np.float32),
        "offs": striped(np.random.permutation(T)[:S]),
        "two": striped(np.random.permutation(T)[:S]),
        "n1": striped8(np.stack([np.random.permutation(S) for _ in range(8)])),
        "n2": striped8(np.stack([np.random.permutation(S) for _ in range(8)])),
        "three": striped(np.random.permutation(T)[:V]),
        "n3": striped8(np.stack([np.random.permutation(V) for _ in range(8)])),
        "n4": striped8(np.stack([np.random.permutation(V) for _ in range(8)])),
        "n5": striped(np.random.randint(0, V, W)),
    }


def reference(x_words, x_scales, w1, w2, sl, th, w3, tau, tau2, ga, gb, tau3, offs, two, n1, n2, three, n3, n4, n5):
    xq = unpack_weight(x_words, x_scales)[:, unstriped(offs)]
    y = mxq(f64(w1), 0, "e4m3").T @ xq
    x_two = unpack_weight(x_words, x_scales)[:, unstriped(two)]
    d = mxq(f64(w2), 0, "e4m3").T @ x_two
    sg = sigmoid(f64(sl) * (d[np.arange(H)[:, None], runs(n1, H)] - f64(th)))
    z = f64(ga) * (y * sg - (0.5 * (y[np.arange(H)[:, None], runs(n2, H)])))
    x_three = unpack_weight(x_words, x_scales)[:, unstriped(three)]
    b = mxq(f64(w3), 0, "e4m3").T @ x_three
    top = b.max(axis=1, keepdims=True)
    ea = np.exp(f64(tau) * (b[np.arange(H)[:, None], runs(n3, H)] - top))
    low = b.min(axis=1, keepdims=True)
    ea2 = np.exp(f64(tau2) * (low - (b[np.arange(H)[:, None], runs(n4, H)])))
    z2 = f64(gb) * (1.5 * (b * (ea + ea2)))
    s = 0.0625 * ((mxq(z, 0, "e4m3").T @ mxq(z2, 0, "e4m3")))
    top2 = s.max(axis=1, keepdims=True)
    ea3 = np.exp(f64(tau3) * (s[:, unstriped(n5)] - top2))
    ms = ea3.reshape(S, V, 4).sum(axis=2)
    return (1.5 * s) / (ms + 0.5)

@@ -1,0 +1,302 @@
+from contextlib import ExitStack
+
+import concourse.mybir as mybir
+from concourse.masks import make_identity
+
+K, T, S, V, H, W = 512, 2048, 512, 256, 512, 1024
+FLOPS = 2 * K * H * (S + S + V) + 2 * H * S * V
+
+F32 = mybir.dt.float32
+BF16 = mybir.dt.bfloat16
+I32 = mybir.dt.int32
+U32 = mybir.dt.uint32
+U16 = mybir.dt.uint16
+U8 = mybir.dt.uint8
+FP8X4 = mybir.dt.float8_e4m3fn_x4
+ALU = mybir.AluOpType
+ACT = mybir.ActivationFunctionType
+AXIS_X = mybir.AxisListType.X
+
+P = 128
+PACK = 4
+HALF = 256
+
+
+def tile_picked_twkgxbedfegs_none_p_kernel(
+    tc, x_words, x_scales, w1, w2, sl, th, w3, tau, tau2, ga, gb, tau3, offs, two, n1, n2, three, n3, n4, n5, out
+):
+    nc = tc.nc
+    with ExitStack() as ctx:
+        keep = ctx.enter_context(tc.tile_pool(name="keep", bufs=1))
+        psum = ctx.enter_context(tc.psum_pool(name="psum", bufs=1))
+
+        def sbuf(name, shape, dtype, tag=None):
+            return keep.tile(shape, dtype, name=name, tag=tag or name, align_bytes=64)
+
+        def bank(name, shape, number):
+            return psum.tile(shape, F32, name=name, tag="bank%d" % number)
+
+        def load_list(name, source):
+            tile = keep.tile(list(source.shape), U16, name=name)
+            nc.sync.dma_start(tile[:], source)
+            return tile
+
+        def load_weight(name, source, cols):
+            tile = sbuf(name, [P, PACK, cols.stop - cols.start], F32)
+            nc.sync.dma_start(tile[:], source.rearrange("(p j) c -> p j c", j=PACK)[:, :, cols])
+            return tile
+
+        def load_rows(name, source):
+            tile = sbuf(name, [P, PACK], F32)
+            nc.sync.dma_start(tile[:], source.rearrange("(p t) o -> p (t o)", t=PACK))
+            return tile
+
+        two_l = load_list("two_l", two)
+        offs_l = load_list("offs_l", offs)
+        words = sbuf("words", [P, T], U32)
+        nc.sync.dma_start(words[:].bitcast(I32), x_words[0].rearrange("p n t -> p (n t)").bitcast(I32))
+        scales = sbuf("scales", [P, T], U8)
+        for q in range(4):
+            nc.scalar.dma_start(
+                scales[32 * q : 32 * q + 32, :].bitcast(I32),
+                x_scales[0, 4 * q : 4 * q + 4, :].bitcast(I32).partition_broadcast(8),
+            )
+        w2_raw = [load_weight("w2_raw%d" % h, w2, slice(HALF * h, HALF * h + HALF)) for h in range(2)]
+        three_l = load_list("three_l", three)
+        n1_l = load_list("n1_l", n1)
+        sl_t = load_rows("sl_t", sl)
+        th_t = load_rows("th_t", th)
+        w1_raw = load_weight("w1_raw", w1, slice(0, H))
+        ga_t = load_rows("ga_t", ga)
+        w3_raw = load_weight("w3_raw", w3, slice(0, H))
+        n2_l = load_list("n2_l", n2)
+        tau_t = load_rows("tau_t", tau)
+        tau2_t = load_rows("tau2_t", tau2)
+        n3_l = load_list("n3_l", n3)
+        n4_l = load_list("n4_l", n4)
+        gb_t = load_rows("gb_t", gb)
+        n5_l = load_list("n5_l", n5)
+        tau3_t = sbuf("tau3_t", [P, 4], F32)
+        with nc.allow_non_contiguous_dma(reason="one value a partition and row tile"):
+            nc.sync.dma_start(tau3_t[:], tau3.rearrange("(m p) o -> p (m o)", p=P))
+
+        ident = sbuf("ident", [P, P], F32)
+        make_identity(nc, ident[:])
+        ds_win = [sbuf("ds_win%d" % t, [P, 2 * S], F32) for t in range(PACK)]
+        b_win = [sbuf("b_win%d" % t, [P, 2 * V], F32) for t in range(PACK)]
+        for t in range(PACK):
+            nc.vector.memset(ds_win[t][:, S:], 0.0)
+        for t in range(PACK):
+            nc.gpsimd.memset(b_win[t][:, V:], 0.0)
+
+        def scaled(name, source, factor):
+            tile = sbuf(name, [P, PACK], F32)
+            nc.gpsimd.tensor_scalar(tile[:], source[:], factor, 0.0, ALU.mult, ALU.add)
+            return tile
+
+        neg_sl = scaled("neg_sl", sl_t, -1.0)
+        sg_bias = sbuf("sg_bias", [P, PACK], F32)
+        nc.gpsimd.tensor_tensor(sg_bias[:], neg_sl[:], th_t[:], ALU.mult)
+        y_gain = scaled("y_gain", ga_t, -0.5)
+        neg_tau = scaled("neg_tau", tau_t, -1.0)
+        neg_tau2 = scaled("neg_tau2", tau2_t, -1.0)
+        b_gain = scaled("b_gain", gb_t, 1.5)
+        neg_tau3 = scaled("neg_tau3", tau3_t, -1.0)
+
+        def gather_packed(name, table, offsets, dtype, tag=None):
+            tile = sbuf(name, [P, 16 * offsets.shape[1]], dtype, tag)
+            nc.vector.tensor_copy(tile[:], table[:].indirect(offsets[:]))
+            return tile
+
+        def deal(grouped, raw, m0):
+            width = raw.shape[2] // PACK
+            dst = grouped[:].rearrange("p (t m j) -> p m j t", t=PACK, j=PACK)[:, m0 : m0 + width]
+            return dst, raw[:].rearrange("p j (m t) -> p m j t", t=PACK)
+
+        def quantise(codes, plane, grouped, c0, c1):
+            nc.vector.quantize_mx(
+                out=codes[:, c0:c1].bitcast(FP8X4), scales=plane[:, c0:c1], in_=grouped[:, PACK * c0 : PACK * c1]
+            )
+
+        def product(acc, codes, plane, t, moving, moving_plane):
+            cols = slice(P * t, P * t + P)
+            nc.tensor.matmul_mx(
+                out=acc,
+                lhsT=codes[:, cols].bitcast(FP8X4),
+                lhsT_scale=plane[:, cols],
+                rhs=moving[:].bitcast(FP8X4),
+                rhs_scale=moving_plane[:],
+                start=True,
+                stop=True,
+            )
+
+        two_b = gather_packed("two_b", scales, two_l, U8)
+        two_w = gather_packed("two_w", words, two_l, U32)
+        offs_b = gather_packed("offs_b", scales, offs_l, U8)
+        three_b = gather_packed("three_b", scales, three_l, U8)
+
+        w2_g = sbuf("w2_g", [P, PACK * H], BF16)
+        nc.scalar.copy(*deal(w2_g, w2_raw[0], 0))
+        nc.vector.tensor_copy(*deal(w2_g, w2_raw[1], 64))
+        w2_c = sbuf("w2_c", [P, H], U32)
+        w2_s = sbuf("w2_s", [P, H], U8)
+        quantise(w2_c, w2_s, w2_g, 0, P)
+        quantise(w2_c, w2_s, w2_g, P, H)
+
+        sg = sbuf("sg", [P, PACK, S], F32)
+        for t in range(PACK):
+            d_ps = bank("d_ps%d" % t, [P, S], t)
+            product(d_ps[:], w2_c, w2_s, t, two_w, two_b)
+            if t == 0:
+                nc.vector.tensor_copy(ds_win[t][:, :S], d_ps[:])
+            else:
+                nc.scalar.copy(ds_win[t][:, :S], d_ps[:])
+            nc.scalar.activation(
+                sg[:, t, :], ds_win[t][:].indirect(n1_l[:]), ACT.Sigmoid,
+                bias=sg_bias[:, t : t + 1], scale=sl_t[:, t : t + 1],
+            )
+
+        offs_w = gather_packed("offs_w", words, offs_l, U32, tag="w2_g")
+        w1_g = sbuf("w1_g", [P, PACK * H], BF16)
+        nc.vector.tensor_copy(*deal(w1_g, w1_raw, 0))
+        w1_c = sbuf("w1_c", [P, H], U32)
+        w1_s = sbuf("w1_s", [P, H], U8)
+        quantise(w1_c, w1_s, w1_g, 0, H)
+        y_win = [sbuf("y_win%d" % t, [P, S], F32) for t in range(PACK)]
+        for t in range(PACK):
+            y_ps = bank("y_ps%d" % t, [P, S], 4 + t)
+            product(y_ps[:], w1_c, w1_s, t, offs_w, offs_b)
+            if t < 2:
+                nc.scalar.activation(y_win[t][:], y_ps[:], ACT.Copy, scale=y_gain[:, t : t + 1])
+            else:
+                nc.vector.tensor_scalar(y_win[t][:], y_ps[:], y_gain[:, t : t + 1], None, ALU.mult)
+
+        three_w = gather_packed("three_w", words, three_l, U32, tag="w1_g")
+        w3_g = sbuf("w3_g", [P, PACK * H], BF16)
+        nc.vector.tensor_copy(*deal(w3_g, w3_raw, 0))
+        w3_c = sbuf("w3_c", [P, H], U32)
+        w3_s = sbuf("w3_s", [P, H], U8)
+        quantise(w3_c, w3_s, w3_g, 0, H)
+        top = sbuf("top", [P, PACK], F32)
+        low = sbuf("low", [P, PACK], F32)
+        ea_bias = [sbuf("ea_bias%d" % u, [P, 2], F32) for u in range(2)]
+        ea2_bias = [sbuf("ea2_bias%d" % u, [P, 2], F32) for u in range(2)]
+        for u in range(2):
+            pair = slice(2 * u, 2 * u + 2)
+            b_ps = bank("b_ps%d" % u, [P, 2, V], u)
+            for e in range(2):
+                product(b_ps[:, e, :], w3_c, w3_s, 2 * u + e, three_w, three_b)
+            for e in range(2):
+                t = 2 * u + e
+                nc.vector.tensor_scalar(
+                    b_win[t][:, :V], b_ps[:, e, :], 1.0, None, ALU.mult, ALU.max, accum_out=top[:, t : t + 1]
+                )
+            nc.vector.tensor_reduce(low[:, pair], b_ps[:], AXIS_X, ALU.min)
+            nc.vector.tensor_tensor(ea_bias[u][:], top[:, pair], neg_tau[:, pair], ALU.mult)
+            nc.vector.tensor_tensor(ea2_bias[u][:], low[:, pair], tau2_t[:, pair], ALU.mult)
+
+        def weave_out(grouped):
+            return grouped[:].rearrange("p (c i t) -> p c t i", i=2, t=PACK)
+
+        def weave_in(planes):
+            return planes.rearrange("p t (c i) -> p c t i", i=2)
+
+        z_g = [sbuf("z_g%d" % m, [P, PACK * P], BF16) for m in range(4)]
+        z_c = [sbuf("z_c%d" % m, [P, P], U32) for m in range(4)]
+        z_s = [sbuf("z_s%d" % m, [P, P], U8) for m in range(4)]
+
+        def gate(m, tag):
+            cols = slice(P * m, P * m + P)
+            gated = sbuf("gated%d" % m, [P, PACK, P], F32, tag)
+            for t in range(PACK):
+                nc.vector.scalar_tensor_tensor(
+                    gated[:, t, :], y_win[t][:, cols], -2.0, sg[:, t, cols], ALU.mult, ALU.mult
+                )
+            return gated
+
+        def z_by_vector(m, tag):
+            gated = gate(m, tag)
+            planes = sbuf("z_planes%d" % m, [P, PACK, P], F32)
+            for t in range(PACK):
+                nc.vector.tensor_tensor(
+                    planes[:, t, :], y_win[t][:].indirect(n2_l[:, 8 * m : 8 * m + 8]), gated[:, t, :], ALU.add
+                )
+            nc.vector.tensor_copy(weave_out(z_g[m]), weave_in(planes[:]))
+            quantise(z_c[m], z_s[m], z_g[m], 0, P)
+
+        z_by_vector(0, "neg_tau")
+
+        ea = sbuf("ea", [P, PACK, V], F32)
+        ea2 = sbuf("ea2", [P, PACK, V], F32)
+        both = sbuf("both", [P, PACK, V], F32)
+        z2 = sbuf("z2", [P, PACK, V], F32)
+        for t in range(PACK):
+            u, e = divmod(t, 2)
+            nc.scalar.activation(
+                ea[:, t, :], b_win[t][:].indirect(n3_l[:]), ACT.Exp,
+                bias=ea_bias[u][:, e : e + 1], scale=tau_t[:, t : t + 1],
+            )
+            nc.scalar.activation(
+                ea2[:, t, :], b_win[t][:].indirect(n4_l[:]), ACT.Exp,
+                bias=ea2_bias[u][:, e : e + 1], scale=neg_tau2[:, t : t + 1],
+            )
+            nc.vector.tensor_tensor(both[:, t, :], ea[:, t, :], ea2[:, t, :], ALU.add)
+            nc.vector.scalar_tensor_tensor(
+                z2[:, t, :], b_win[t][:, :V], b_gain[:, t : t + 1], both[:, t, :], ALU.mult, ALU.mult
+            )
+        z2_g = sbuf("z2_g", [P, PACK * V], BF16)
+        z2_c = sbuf("z2_c", [P, V], U32)
+        z2_s = sbuf("z2_s", [P, V], U8)
+        nc.vector.tensor_copy(weave_out(z2_g), weave_in(z2[:]))
+        quantise(z2_c, z2_s, z2_g, 0, V)
+
+        picked = sbuf("picked", [P, PACK, 2 * P], F32, tag="ea2_bias1")
+        for t in range(PACK):
+            nc.scalar.activation(picked[:, t, :], y_win[t][:].indirect(n2_l[:, 8:24]), ACT.Copy)
+
+        def z_from_picked(m, tag):
+            gated = gate(m, tag)
+            cols = slice(P * (m - 1), P * m)
+            nc.vector.tensor_tensor(weave_out(z_g[m]), weave_in(picked[:, :, cols]), weave_in(gated[:]), ALU.add)
+            quantise(z_c[m], z_s[m], z_g[m], 0, P)
+
+        top2 = sbuf("top2", [P, 4], F32)
+        ea3_bias = sbuf("ea3_bias", [P, 4], F32)
+        for m in range(4):
+            if m == 1:
+                z_from_picked(1, "z2_g")
+            if m == 2:
+                z_from_picked(2, "z_g1")
+            if m == 3:
+                z_by_vector(3, "z_g2")
+            s_ps = bank("s_ps%d" % m, [P, V], m)
+            product(s_ps[:], z_c[m], z_s[m], 0, z2_c, z2_s)
+            nc.vector.tensor_scalar(
+                ds_win[m][:, :V], s_ps[:], 0.0625, None, ALU.mult, ALU.max, accum_out=top2[:, m : m + 1]
+            )
+            nc.vector.tensor_tensor(ea3_bias[:, m : m + 1], top2[:, m : m + 1], neg_tau3[:, m : m + 1], ALU.mult)
+        sums = [bank("sums%d" % m, [P, 2, P], (m + 1) % 4) for m in range(4)]
+        for m in range(4):
+            for g in range(2):
+                ea3 = sbuf("ea3_%d_%d" % (m, g), [P, 512], F32)
+                nc.scalar.activation(
+                    ea3[:], ds_win[m][:].indirect(n5_l[:, 32 * g : 32 * g + 32]), ACT.Exp,
+                    bias=ea3_bias[:, m : m + 1], scale=tau3_t[:, m : m + 1],
+                )
+                for member in range(4):
+                    nc.tensor.matmul(
+                        sums[m][:, g, :], ea3[:, member::4], ident[:],
+                        is_transpose=True, start=(member == 0), stop=(member == 3),
+                    )
+
+        root = sbuf("root", [P, 4, 2, P], F32, tag="ea3_bias")
+        for m in range(4):
+            nc.scalar.activation(root[:, m], sums[m][:], ACT.Abs_reciprocal_sqrt, bias=0.5)
+            root_ps = bank("root_ps%d" % m, [P, V], 4 + m)
+            for g in range(2):
+                nc.tensor.transpose(root_ps[:, P * g : P * g + P], root[:, m, g, :], ident[:])
+            once = sbuf("once%d" % m, [P, V], F32)
+            nc.vector.scalar_tensor_tensor(once[:], ds_win[m][:, :V], 1.5, root_ps[:], ALU.mult, ALU.mult)
+            result = sbuf("result%d" % m, [P, V], F32)
+            nc.vector.tensor_tensor(result[:], once[:], root_ps[:], ALU.mult)
+            nc.sync.dma_start(out[P * m : P * m + P, :], result[:])

@@ -53,27 +53,27 @@ def tile_picked_twkgxbedfegs_none_p_kernel(
 
         two_l = load_list("two_l", two)
         offs_l = load_list("offs_l", offs)
-        words = sbuf("words", [P, T], U32)
-        nc.sync.dma_start(words[:].bitcast(I32), x_words[0].rearrange("p n t -> p (n t)").bitcast(I32))
+        n1_l = load_list("n1_l", n1)
         scales = sbuf("scales", [P, T], U8)
         for q in range(4):
-            nc.scalar.dma_start(
+            nc.sync.dma_start(
                 scales[32 * q : 32 * q + 32, :].bitcast(I32),
                 x_scales[0, 4 * q : 4 * q + 4, :].bitcast(I32).partition_broadcast(8),
             )
-        w2_raw = [load_weight("w2_raw%d" % h, w2, slice(HALF * h, HALF * h + HALF)) for h in range(2)]
-        three_l = load_list("three_l", three)
-        n1_l = load_list("n1_l", n1)
+        words = sbuf("words", [P, T], U32)
+        nc.sync.dma_start(words[:].bitcast(I32), x_words[0].rearrange("p n t -> p (n t)").bitcast(I32))
         sl_t = load_rows("sl_t", sl)
         th_t = load_rows("th_t", th)
+        w2_raw = [load_weight("w2_raw0", w2, slice(0, 192)), load_weight("w2_raw1", w2, slice(192, H))]
+        n3_l = load_list("n3_l", n3)
+        three_l = load_list("three_l", three)
+        w3_raw = load_weight("w3_raw", w3, slice(0, H))
+        tau2_t = load_rows("tau2_t", tau2)
         w1_raw = load_weight("w1_raw", w1, slice(0, H))
         ga_t = load_rows("ga_t", ga)
-        w3_raw = load_weight("w3_raw", w3, slice(0, H))
+        n4_l = load_list("n4_l", n4)
         n2_l = load_list("n2_l", n2)
         tau_t = load_rows("tau_t", tau)
-        tau2_t = load_rows("tau2_t", tau2)
-        n3_l = load_list("n3_l", n3)
-        n4_l = load_list("n4_l", n4)
         gb_t = load_rows("gb_t", gb)
         n5_l = load_list("n5_l", n5)
         tau3_t = sbuf("tau3_t", [P, 4], F32)
@@ -87,18 +87,16 @@ def tile_picked_twkgxbedfegs_none_p_kernel(
         for t in range(PACK):
             nc.vector.memset(ds_win[t][:, S:], 0.0)
         for t in range(PACK):
-            nc.gpsimd.memset(b_win[t][:, V:], 0.0)
+            nc.vector.memset(b_win[t][:, V:], 0.0)
+        halves = sbuf("halves", [P, P], F32)
+        nc.gpsimd.memset(halves[:], 0.5)
 
         def scaled(name, source, factor):
             tile = sbuf(name, [P, PACK], F32)
             nc.gpsimd.tensor_scalar(tile[:], source[:], factor, 0.0, ALU.mult, ALU.add)
             return tile
 
-        neg_sl = scaled("neg_sl", sl_t, -1.0)
-        sg_bias = sbuf("sg_bias", [P, PACK], F32)
-        nc.gpsimd.tensor_tensor(sg_bias[:], neg_sl[:], th_t[:], ALU.mult)
         y_gain = scaled("y_gain", ga_t, -0.5)
-        neg_tau = scaled("neg_tau", tau_t, -1.0)
         neg_tau2 = scaled("neg_tau2", tau2_t, -1.0)
         b_gain = scaled("b_gain", gb_t, 1.5)
         neg_tau3 = scaled("neg_tau3", tau3_t, -1.0)
@@ -110,8 +108,8 @@ def tile_picked_twkgxbedfegs_none_p_kernel(
 
         def deal(grouped, raw, m0):
             width = raw.shape[2] // PACK
-            dst = grouped[:].rearrange("p (t m j) -> p m j t", t=PACK, j=PACK)[:, m0 : m0 + width]
-            return dst, raw[:].rearrange("p j (m t) -> p m j t", t=PACK)
+            dst = grouped[:].rearrange("p (t m j) -> p m t j", t=PACK, j=PACK)[:, m0 : m0 + width]
+            return dst, raw[:].rearrange("p j (m t) -> p m t j", t=PACK)
 
         def quantise(codes, plane, grouped, c0, c1):
             nc.vector.quantize_mx(
@@ -133,67 +131,75 @@ def tile_picked_twkgxbedfegs_none_p_kernel(
         two_b = gather_packed("two_b", scales, two_l, U8)
         two_w = gather_packed("two_w", words, two_l, U32)
         offs_b = gather_packed("offs_b", scales, offs_l, U8)
-        three_b = gather_packed("three_b", scales, three_l, U8)
 
         w2_g = sbuf("w2_g", [P, PACK * H], BF16)
         nc.scalar.copy(*deal(w2_g, w2_raw[0], 0))
-        nc.vector.tensor_copy(*deal(w2_g, w2_raw[1], 64))
+        neg_sl = sbuf("neg_sl", [P, PACK], F32)
+        nc.scalar.activation(neg_sl[:], sl_t[:], ACT.Copy, scale=-1.0)
+        nc.vector.tensor_copy(*deal(w2_g, w2_raw[1], 48))
+        sg_bias = sbuf("sg_bias", [P, PACK], F32)
+        nc.vector.tensor_tensor(sg_bias[:], neg_sl[:], th_t[:], ALU.mult)
+        w2_c0 = sbuf("w2_c0", [P, P], U32)
+        w2_s0 = sbuf("w2_s0", [P, P], U8)
         w2_c = sbuf("w2_c", [P, H], U32)
         w2_s = sbuf("w2_s", [P, H], U8)
-        quantise(w2_c, w2_s, w2_g, 0, P)
+        quantise(w2_c0, w2_s0, w2_g, 0, P)
         quantise(w2_c, w2_s, w2_g, P, H)
 
         sg = sbuf("sg", [P, PACK, S], F32)
         for t in range(PACK):
-            d_ps = bank("d_ps%d" % t, [P, S], t)
-            product(d_ps[:], w2_c, w2_s, t, two_w, two_b)
+            d_ps = bank("d_ps%d" % t, [P, S], 0)
             if t == 0:
+                product(d_ps[:], w2_c0, w2_s0, t, two_w, two_b)
                 nc.vector.tensor_copy(ds_win[t][:, :S], d_ps[:])
             else:
+                product(d_ps[:], w2_c, w2_s, t, two_w, two_b)
                 nc.scalar.copy(ds_win[t][:, :S], d_ps[:])
             nc.scalar.activation(
                 sg[:, t, :], ds_win[t][:].indirect(n1_l[:]), ACT.Sigmoid,
                 bias=sg_bias[:, t : t + 1], scale=sl_t[:, t : t + 1],
             )
 
-        offs_w = gather_packed("offs_w", words, offs_l, U32, tag="w2_g")
+        neg_tau = sbuf("neg_tau", [P, PACK], F32, tag="sg_bias")
+        nc.scalar.activation(neg_tau[:], tau_t[:], ACT.Copy, scale=-1.0)
+        three_b = gather_packed("three_b", scales, three_l, U8, tag="w2_g")
+        three_w = gather_packed("three_w", words, three_l, U32, tag="w2_s0")
+        w3_g = sbuf("w3_g", [P, PACK * H], BF16)
+        nc.vector.tensor_copy(*deal(w3_g, w3_raw, 0))
+        offs_w = gather_packed("offs_w", words, offs_l, U32, tag="w2_c0")
+        w3_c = sbuf("w3_c", [P, H], U32)
+        w3_s = sbuf("w3_s", [P, H], U8)
+        quantise(w3_c, w3_s, w3_g, 0, H)
+        b_ps = [bank("b_ps%d" % u, [P, 2, V], 2 + u) for u in range(2)]
+        for t in range(PACK):
+            product(b_ps[t // 2][:, t % 2, :], w3_c, w3_s, t, three_w, three_b)
         w1_g = sbuf("w1_g", [P, PACK * H], BF16)
         nc.vector.tensor_copy(*deal(w1_g, w1_raw, 0))
         w1_c = sbuf("w1_c", [P, H], U32)
         w1_s = sbuf("w1_s", [P, H], U8)
-        quantise(w1_c, w1_s, w1_g, 0, H)
-        y_win = [sbuf("y_win%d" % t, [P, S], F32) for t in range(PACK)]
-        for t in range(PACK):
-            y_ps = bank("y_ps%d" % t, [P, S], 4 + t)
-            product(y_ps[:], w1_c, w1_s, t, offs_w, offs_b)
-            if t < 2:
-                nc.scalar.activation(y_win[t][:], y_ps[:], ACT.Copy, scale=y_gain[:, t : t + 1])
-            else:
-                nc.vector.tensor_scalar(y_win[t][:], y_ps[:], y_gain[:, t : t + 1], None, ALU.mult)
-
-        three_w = gather_packed("three_w", words, three_l, U32, tag="w1_g")
-        w3_g = sbuf("w3_g", [P, PACK * H], BF16)
-        nc.vector.tensor_copy(*deal(w3_g, w3_raw, 0))
-        w3_c = sbuf("w3_c", [P, H], U32)
-        w3_s = sbuf("w3_s", [P, H], U8)
-        quantise(w3_c, w3_s, w3_g, 0, H)
         top = sbuf("top", [P, PACK], F32)
         low = sbuf("low", [P, PACK], F32)
         ea_bias = [sbuf("ea_bias%d" % u, [P, 2], F32) for u in range(2)]
         ea2_bias = [sbuf("ea2_bias%d" % u, [P, 2], F32) for u in range(2)]
+        y_ps = [bank("y_ps%d" % t, [P, S], 4 + t) for t in range(PACK)]
         for u in range(2):
             pair = slice(2 * u, 2 * u + 2)
-            b_ps = bank("b_ps%d" % u, [P, 2, V], u)
-            for e in range(2):
-                product(b_ps[:, e, :], w3_c, w3_s, 2 * u + e, three_w, three_b)
             for e in range(2):
                 t = 2 * u + e
                 nc.vector.tensor_scalar(
-                    b_win[t][:, :V], b_ps[:, e, :], 1.0, None, ALU.mult, ALU.max, accum_out=top[:, t : t + 1]
+                    b_win[t][:, :V], b_ps[u][:, e, :], 1.0, None, ALU.mult, ALU.max, accum_out=top[:, t : t + 1]
                 )
-            nc.vector.tensor_reduce(low[:, pair], b_ps[:], AXIS_X, ALU.min)
+                if t == 0:
+                    quantise(w1_c, w1_s, w1_g, 0, H)
+                    for r in range(PACK):
+                        product(y_ps[r][:], w1_c, w1_s, r, offs_w, offs_b)
+            nc.vector.tensor_reduce(low[:, pair], b_ps[u][:], AXIS_X, ALU.min)
             nc.vector.tensor_tensor(ea_bias[u][:], top[:, pair], neg_tau[:, pair], ALU.mult)
             nc.vector.tensor_tensor(ea2_bias[u][:], low[:, pair], tau2_t[:, pair], ALU.mult)
+        y_win = [sbuf("y_win%d" % t, [P, S], F32) for t in range(PACK)]
+
+        def y_out(t):
+            nc.vector.tensor_scalar(y_win[t][:], y_ps[t][:], y_gain[:, t : t + 1], None, ALU.mult)
 
         def weave_out(grouped):
             return grouped[:].rearrange("p (c i t) -> p c t i", i=2, t=PACK)
@@ -205,26 +211,17 @@ def tile_picked_twkgxbedfegs_none_p_kernel(
         z_c = [sbuf("z_c%d" % m, [P, P], U32) for m in range(4)]
         z_s = [sbuf("z_s%d" % m, [P, P], U8) for m in range(4)]
 
-        def gate(m, tag):
-            cols = slice(P * m, P * m + P)
-            gated = sbuf("gated%d" % m, [P, PACK, P], F32, tag)
-            for t in range(PACK):
-                nc.vector.scalar_tensor_tensor(
-                    gated[:, t, :], y_win[t][:, cols], -2.0, sg[:, t, cols], ALU.mult, ALU.mult
-                )
-            return gated
+        def gate(gated, cols, t):
+            nc.vector.scalar_tensor_tensor(gated[:, t, :], y_win[t][:, cols], -2.0, sg[:, t, cols], ALU.mult, ALU.mult)
 
-        def z_by_vector(m, tag):
-            gated = gate(m, tag)
-            planes = sbuf("z_planes%d" % m, [P, PACK, P], F32)
-            for t in range(PACK):
-                nc.vector.tensor_tensor(
-                    planes[:, t, :], y_win[t][:].indirect(n2_l[:, 8 * m : 8 * m + 8]), gated[:, t, :], ALU.add
-                )
-            nc.vector.tensor_copy(weave_out(z_g[m]), weave_in(planes[:]))
+        def add_picked(m, gated):
+            h, e = divmod(m, 2)
+            nc.vector.tensor_tensor(
+                weave_out(z_g[m]), weave_in(picked[:, h, :, P * e : P * e + P]), weave_in(gated), ALU.add
+            )
+
+        def quantise_z(m):
             quantise(z_c[m], z_s[m], z_g[m], 0, P)
-
-        z_by_vector(0, "neg_tau")
 
         ea = sbuf("ea", [P, PACK, V], F32)
         ea2 = sbuf("ea2", [P, PACK, V], F32)
@@ -240,63 +237,129 @@ def tile_picked_twkgxbedfegs_none_p_kernel(
                 ea2[:, t, :], b_win[t][:].indirect(n4_l[:]), ACT.Exp,
                 bias=ea2_bias[u][:, e : e + 1], scale=neg_tau2[:, t : t + 1],
             )
+
+        def add_both(t):
             nc.vector.tensor_tensor(both[:, t, :], ea[:, t, :], ea2[:, t, :], ALU.add)
+
+        def weigh(t):
             nc.vector.scalar_tensor_tensor(
                 z2[:, t, :], b_win[t][:, :V], b_gain[:, t : t + 1], both[:, t, :], ALU.mult, ALU.mult
             )
+
+        y_out(0)
+        y_out(1)
+        add_both(0)
+        y_out(2)
+        weigh(0)
+        add_both(1)
+        y_out(3)
+        picked = sbuf("picked", [P, 2, PACK, HALF], F32, "ea2_bias1")
+        for h in range(2):
+            for t in range(PACK):
+                nc.scalar.activation(picked[:, h, t, :], y_win[t][:].indirect(n2_l[:, 16 * h : 16 * h + 16]), ACT.Copy)
+
+        first, second, rest = slice(0, P), slice(P, HALF), slice(HALF, S)
+        gated0 = sbuf("gated0", [P, PACK, P], F32, "sg_bias")
+        weigh(1)
+        add_both(2)
+        gate(gated0, first, 0)
+        weigh(2)
+        add_both(3)
+        gate(gated0, first, 1)
+        weigh(3)
+        gate(gated0, first, 2)
         z2_g = sbuf("z2_g", [P, PACK * V], BF16)
         z2_c = sbuf("z2_c", [P, V], U32)
         z2_s = sbuf("z2_s", [P, V], U8)
         nc.vector.tensor_copy(weave_out(z2_g), weave_in(z2[:]))
+        gate(gated0, first, 3)
         quantise(z2_c, z2_s, z2_g, 0, V)
-
-        picked = sbuf("picked", [P, PACK, 2 * P], F32, tag="ea2_bias1")
-        for t in range(PACK):
-            nc.scalar.activation(picked[:, t, :], y_win[t][:].indirect(n2_l[:, 8:24]), ACT.Copy)
-
-        def z_from_picked(m, tag):
-            gated = gate(m, tag)
-            cols = slice(P * (m - 1), P * m)
-            nc.vector.tensor_tensor(weave_out(z_g[m]), weave_in(picked[:, :, cols]), weave_in(gated[:]), ALU.add)
-            quantise(z_c[m], z_s[m], z_g[m], 0, P)
+        add_picked(0, gated0[:])
+        gated1 = sbuf("gated1", [P, PACK, P], F32, "both")
+        gate(gated1, second, 0)
+        quantise_z(0)
 
         top2 = sbuf("top2", [P, 4], F32)
         ea3_bias = sbuf("ea3_bias", [P, 4], F32)
-        for m in range(4):
-            if m == 1:
-                z_from_picked(1, "z2_g")
-            if m == 2:
-                z_from_picked(2, "z_g1")
-            if m == 3:
-                z_by_vector(3, "z_g2")
+
+        def scores(m):
             s_ps = bank("s_ps%d" % m, [P, V], m)
             product(s_ps[:], z_c[m], z_s[m], 0, z2_c, z2_s)
             nc.vector.tensor_scalar(
                 ds_win[m][:, :V], s_ps[:], 0.0625, None, ALU.mult, ALU.max, accum_out=top2[:, m : m + 1]
             )
+
+        def scores_bias(m):
             nc.vector.tensor_tensor(ea3_bias[:, m : m + 1], top2[:, m : m + 1], neg_tau3[:, m : m + 1], ALU.mult)
-        sums = [bank("sums%d" % m, [P, 2, P], (m + 1) % 4) for m in range(4)]
+
+        gated23 = sbuf("gated23", [P, PACK, HALF], F32, "z2_g")
+        gate(gated1, second, 1)
+        gate(gated1, second, 2)
+        scores(0)
+        gate(gated1, second, 3)
+        scores_bias(0)
+        add_picked(1, gated1[:])
+        gate(gated23, rest, 0)
+        quantise_z(1)
+        gate(gated23, rest, 1)
+        scores(1)
+        gate(gated23, rest, 2)
+        scores_bias(1)
+        gate(gated23, rest, 3)
+        add_picked(2, gated23[:, :, :P])
+        add_picked(3, gated23[:, :, P:])
+        quantise_z(2)
+        quantise_z(3)
+        scores(2)
+        scores(3)
+        scores_bias(2)
+        scores_bias(3)
+
+        sums_ps = [bank("sums_ps%d" % m, [P, 2, P], m + 1) for m in range(2)]
+        ea3 = [sbuf("ea3_%d" % m, [P, W], F32) for m in range(4)]
         for m in range(4):
             for g in range(2):
-                ea3 = sbuf("ea3_%d_%d" % (m, g), [P, 512], F32)
                 nc.scalar.activation(
-                    ea3[:], ds_win[m][:].indirect(n5_l[:, 32 * g : 32 * g + 32]), ACT.Exp,
+                    ea3[m][:, 512 * g : 512 * g + 512], ds_win[m][:].indirect(n5_l[:, 32 * g : 32 * g + 32]), ACT.Exp,
                     bias=ea3_bias[:, m : m + 1], scale=tau3_t[:, m : m + 1],
                 )
-                for member in range(4):
-                    nc.tensor.matmul(
-                        sums[m][:, g, :], ea3[:, member::4], ident[:],
-                        is_transpose=True, start=(member == 0), stop=(member == 3),
-                    )
+                if m < 2:
+                    terms = [ea3[m][:, 512 * g + member : 512 * g + 512 : 4] for member in range(4)]
+                    if m == 0:
+                        terms.append(halves[:])
+                    for place, term in enumerate(terms):
+                        nc.tensor.matmul(
+                            sums_ps[m][:, g, :], term, ident[:],
+                            is_transpose=True, start=(place == 0), stop=(place == len(terms) - 1),
+                        )
 
-        root = sbuf("root", [P, 4, 2, P], F32, tag="ea3_bias")
-        for m in range(4):
-            nc.scalar.activation(root[:, m], sums[m][:], ACT.Abs_reciprocal_sqrt, bias=0.5)
-            root_ps = bank("root_ps%d" % m, [P, V], 4 + m)
+        def turn_back_and_store(m, inverse):
+            inverse_ps = bank("inverse_ps%d" % m, [P, V], 4 + m)
             for g in range(2):
-                nc.tensor.transpose(root_ps[:, P * g : P * g + P], root[:, m, g, :], ident[:])
-            once = sbuf("once%d" % m, [P, V], F32)
-            nc.vector.scalar_tensor_tensor(once[:], ds_win[m][:, :V], 1.5, root_ps[:], ALU.mult, ALU.mult)
+                nc.tensor.transpose(inverse_ps[:, P * g : P * g + P], inverse[:, P * g : P * g + P], ident[:])
             result = sbuf("result%d" % m, [P, V], F32)
-            nc.vector.tensor_tensor(result[:], once[:], root_ps[:], ALU.mult)
+            nc.vector.scalar_tensor_tensor(result[:], ds_win[m][:, :V], 1.5, inverse_ps[:], ALU.mult, ALU.mult)
             nc.sync.dma_start(out[P * m : P * m + P, :], result[:])
+
+        inverse0 = sbuf("inverse0", [P, V], F32, tag="neg_tau3")
+        nc.vector.reciprocal(inverse0[:], sums_ps[0][:].rearrange("p g i -> p (g i)"))
+        sums = sbuf("sums", [P, 2, V], F32, tag="top2")
+        nc.vector.tensor_reduce(sums[:, 0, :], ea3[2][:].rearrange("p (v d) -> p v d", d=4), AXIS_X, ALU.add)
+        turn_back_and_store(0, inverse0)
+        nc.vector.tensor_reduce(sums[:, 1, :], ea3[3][:].rearrange("p (v d) -> p v d", d=4), AXIS_X, ALU.add)
+        root = sbuf("root", [P, 4, V], F32, tag="ea3_bias")
+        once = {}
+        for m in (2, 3):
+            nc.scalar.activation(root[:, m, :], sums[:, m - 2, :], ACT.Abs_reciprocal_sqrt, bias=0.5)
+            once[m] = sbuf("once%d" % m, [P, V], F32)
+            nc.vector.scalar_tensor_tensor(once[m][:], ds_win[m][:, :V], 1.5, root[:, m, :], ALU.mult, ALU.mult)
+        for m in (2, 3):
+            result = sbuf("result%d" % m, [P, V], F32)
+            nc.vector.tensor_tensor(result[:], once[m][:], root[:, m, :], ALU.mult)
+            nc.sync.dma_start(out[P * m : P * m + P, :], result[:])
+        nc.scalar.activation(
+            root[:, 1, :], sums_ps[1][:].rearrange("p g i -> p (g i)"), ACT.Abs_reciprocal_sqrt, bias=0.5
+        )
+        inverse1 = sbuf("inverse1", [P, V], F32)
+        nc.scalar.activation(inverse1[:], root[:, 1, :], ACT.Square)
+        turn_back_and_store(1, inverse1)

@@ -96,7 +96,6 @@ def tile_picked_twkgxbedfegs_none_p_kernel(
             nc.gpsimd.tensor_scalar(tile[:], source[:], factor, 0.0, ALU.mult, ALU.add)
             return tile
 
-        y_gain = scaled("y_gain", ga_t, -0.5)
         neg_tau2 = scaled("neg_tau2", tau2_t, -1.0)
         b_gain = scaled("b_gain", gb_t, 1.5)
         neg_tau3 = scaled("neg_tau3", tau3_t, -1.0)
@@ -177,8 +176,8 @@ def tile_picked_twkgxbedfegs_none_p_kernel(
         nc.vector.tensor_copy(*deal(w1_g, w1_raw, 0))
         w1_c = sbuf("w1_c", [P, H], U32)
         w1_s = sbuf("w1_s", [P, H], U8)
-        top = sbuf("top", [P, PACK], F32)
-        low = sbuf("low", [P, PACK], F32)
+        extremes = sbuf("extremes", [P, 2, PACK], F32, tag="w1_raw")
+        top, low = extremes[:, 0, :], extremes[:, 1, :]
         ea_bias = [sbuf("ea_bias%d" % u, [P, 2], F32) for u in range(2)]
         ea2_bias = [sbuf("ea2_bias%d" % u, [P, 2], F32) for u in range(2)]
         y_ps = [bank("y_ps%d" % t, [P, S], 4 + t) for t in range(PACK)]
@@ -199,7 +198,7 @@ def tile_picked_twkgxbedfegs_none_p_kernel(
         y_win = [sbuf("y_win%d" % t, [P, S], F32) for t in range(PACK)]
 
         def y_out(t):
-            nc.vector.tensor_scalar(y_win[t][:], y_ps[t][:], y_gain[:, t : t + 1], None, ALU.mult)
+            nc.vector.tensor_scalar(y_win[t][:], y_ps[t][:], ga_t[:, t : t + 1], None, ALU.mult)
 
         def weave_out(grouped):
             return grouped[:].rearrange("p (c i t) -> p c t i", i=2, t=PACK)
@@ -211,13 +210,17 @@ def tile_picked_twkgxbedfegs_none_p_kernel(
         z_c = [sbuf("z_c%d" % m, [P, P], U32) for m in range(4)]
         z_s = [sbuf("z_s%d" % m, [P, P], U8) for m in range(4)]
 
-        def gate(gated, cols, t):
-            nc.vector.scalar_tensor_tensor(gated[:, t, :], y_win[t][:, cols], -2.0, sg[:, t, cols], ALU.mult, ALU.mult)
+        def gate(h, t):
+            cols = slice(HALF * h, HALF * h + HALF)
+            nc.vector.scalar_tensor_tensor(
+                gated[h][:, t, :], y_ps[t][:, cols], ga_t[:, t : t + 1], sg[:, t, cols], ALU.mult, ALU.mult
+            )
 
-        def add_picked(m, gated):
+        def add_picked(m):
             h, e = divmod(m, 2)
             nc.vector.tensor_tensor(
-                weave_out(z_g[m]), weave_in(picked[:, h, :, P * e : P * e + P]), weave_in(gated), ALU.add
+                weave_out(z_g[m]), weave_in(picked[:, h, :, P * e : P * e + P]),
+                weave_in(gated[h][:, :, P * e : P * e + P]), ALU.add,
             )
 
         def quantise_z(m):
@@ -238,45 +241,41 @@ def tile_picked_twkgxbedfegs_none_p_kernel(
                 bias=ea2_bias[u][:, e : e + 1], scale=neg_tau2[:, t : t + 1],
             )
 
-        def add_both(t):
-            nc.vector.tensor_tensor(both[:, t, :], ea[:, t, :], ea2[:, t, :], ALU.add)
+        for t in range(PACK):
+            nc.gpsimd.tensor_tensor(both[:, t, :], ea[:, t, :], ea2[:, t, :], ALU.add)
 
         def weigh(t):
             nc.vector.scalar_tensor_tensor(
-                z2[:, t, :], b_win[t][:, :V], b_gain[:, t : t + 1], both[:, t, :], ALU.mult, ALU.mult
+                z2[:, t, :], b_ps[t // 2][:, t % 2, :], b_gain[:, t : t + 1], both[:, t, :], ALU.mult, ALU.mult
             )
 
+        gated = [sbuf("gated0", [P, PACK, HALF], F32, "sg_bias")]
         y_out(0)
         y_out(1)
-        add_both(0)
-        y_out(2)
+        gate(0, 0)
         weigh(0)
-        add_both(1)
+        y_out(2)
+        gate(0, 1)
+        weigh(1)
         y_out(3)
+        gate(0, 2)
+        weigh(2)
+        gate(0, 3)
+        weigh(3)
+        gated.append(sbuf("gated1", [P, PACK, HALF], F32, "ea"))
         picked = sbuf("picked", [P, 2, PACK, HALF], F32, "ea2_bias1")
         for h in range(2):
             for t in range(PACK):
-                nc.scalar.activation(picked[:, h, t, :], y_win[t][:].indirect(n2_l[:, 16 * h : 16 * h + 16]), ACT.Copy)
-
-        first, second, rest = slice(0, P), slice(P, HALF), slice(HALF, S)
-        gated0 = sbuf("gated0", [P, PACK, P], F32, "sg_bias")
-        weigh(1)
-        add_both(2)
-        gate(gated0, first, 0)
-        weigh(2)
-        add_both(3)
-        gate(gated0, first, 1)
-        weigh(3)
-        gate(gated0, first, 2)
+                nc.scalar.activation(
+                    picked[:, h, t, :], y_win[t][:].indirect(n2_l[:, 16 * h : 16 * h + 16]), ACT.Copy, scale=-0.5
+                )
         z2_g = sbuf("z2_g", [P, PACK * V], BF16)
         z2_c = sbuf("z2_c", [P, V], U32)
         z2_s = sbuf("z2_s", [P, V], U8)
+        gate(1, 0)
         nc.vector.tensor_copy(weave_out(z2_g), weave_in(z2[:]))
-        gate(gated0, first, 3)
+        add_picked(0)
         quantise(z2_c, z2_s, z2_g, 0, V)
-        add_picked(0, gated0[:])
-        gated1 = sbuf("gated1", [P, PACK, P], F32, "both")
-        gate(gated1, second, 0)
         quantise_z(0)
 
         top2 = sbuf("top2", [P, 4], F32)
@@ -292,22 +291,17 @@ def tile_picked_twkgxbedfegs_none_p_kernel(
         def scores_bias(m):
             nc.vector.tensor_tensor(ea3_bias[:, m : m + 1], top2[:, m : m + 1], neg_tau3[:, m : m + 1], ALU.mult)
 
-        gated23 = sbuf("gated23", [P, PACK, HALF], F32, "z2_g")
-        gate(gated1, second, 1)
-        gate(gated1, second, 2)
+        add_picked(1)
         scores(0)
-        gate(gated1, second, 3)
-        scores_bias(0)
-        add_picked(1, gated1[:])
-        gate(gated23, rest, 0)
         quantise_z(1)
-        gate(gated23, rest, 1)
+        scores_bias(0)
+        gate(1, 1)
+        gate(1, 2)
         scores(1)
-        gate(gated23, rest, 2)
+        gate(1, 3)
         scores_bias(1)
-        gate(gated23, rest, 3)
-        add_picked(2, gated23[:, :, :P])
-        add_picked(3, gated23[:, :, P:])
+        add_picked(2)
+        add_picked(3)
         quantise_z(2)
         quantise_z(3)
         scores(2)

from contextlib import ExitStack

import concourse.mybir as mybir
from concourse.masks import make_identity

K, T, S, V, H, W = 512, 2048, 512, 256, 512, 1024
FLOPS = 2 * K * H * (S + S + V) + 2 * H * S * V

F32 = mybir.dt.float32
BF16 = mybir.dt.bfloat16
I32 = mybir.dt.int32
U32 = mybir.dt.uint32
U16 = mybir.dt.uint16
U8 = mybir.dt.uint8
FP8X4 = mybir.dt.float8_e4m3fn_x4
ALU = mybir.AluOpType
ACT = mybir.ActivationFunctionType
AXIS_X = mybir.AxisListType.X

P = 128
PACK = 4
HALF = 256


def tile_picked_twkgxbedfegs_none_p_kernel(
    tc, x_words, x_scales, w1, w2, sl, th, w3, tau, tau2, ga, gb, tau3, offs, two, n1, n2, three, n3, n4, n5, out
):
    nc = tc.nc
    with ExitStack() as ctx:
        keep = ctx.enter_context(tc.tile_pool(name="keep", bufs=1))
        psum = ctx.enter_context(tc.psum_pool(name="psum", bufs=1))

        def sbuf(name, shape, dtype, tag=None):
            return keep.tile(shape, dtype, name=name, tag=tag or name, align_bytes=64)

        def bank(name, shape, number):
            return psum.tile(shape, F32, name=name, tag="bank%d" % number)

        def load_list(name, source):
            tile = keep.tile(list(source.shape), U16, name=name)
            nc.sync.dma_start(tile[:], source)
            return tile

        def load_weight(name, source, cols):
            tile = sbuf(name, [P, PACK, cols.stop - cols.start], F32)
            nc.sync.dma_start(tile[:], source.rearrange("(p j) c -> p j c", j=PACK)[:, :, cols])
            return tile

        def load_rows(name, source):
            tile = sbuf(name, [P, PACK], F32)
            nc.sync.dma_start(tile[:], source.rearrange("(p t) o -> p (t o)", t=PACK))
            return tile

        two_l = load_list("two_l", two)
        offs_l = load_list("offs_l", offs)
        n1_l = load_list("n1_l", n1)
        scales = sbuf("scales", [P, T], U8)
        for q in range(4):
            nc.sync.dma_start(
                scales[32 * q : 32 * q + 32, :].bitcast(I32),
                x_scales[0, 4 * q : 4 * q + 4, :].bitcast(I32).partition_broadcast(8),
            )
        words = sbuf("words", [P, T], U32)
        nc.sync.dma_start(words[:].bitcast(I32), x_words[0].rearrange("p n t -> p (n t)").bitcast(I32))
        sl_t = load_rows("sl_t", sl)
        th_t = load_rows("th_t", th)
        w2_raw = [load_weight("w2_raw0", w2, slice(0, 192)), load_weight("w2_raw1", w2, slice(192, H))]
        n3_l = load_list("n3_l", n3)
        three_l = load_list("three_l", three)
        w3_raw = load_weight("w3_raw", w3, slice(0, H))
        tau2_t = load_rows("tau2_t", tau2)
        w1_raw = load_weight("w1_raw", w1, slice(0, H))
        ga_t = load_rows("ga_t", ga)
        n4_l = load_list("n4_l", n4)
        n2_l = load_list("n2_l", n2)
        tau_t = load_rows("tau_t", tau)
        gb_t = load_rows("gb_t", gb)
        n5_l = load_list("n5_l", n5)
        tau3_t = sbuf("tau3_t", [P, 4], F32)
        with nc.allow_non_contiguous_dma(reason="one value a partition and row tile"):
            nc.sync.dma_start(tau3_t[:], tau3.rearrange("(m p) o -> p (m o)", p=P))

        ident = sbuf("ident", [P, P], F32)
        make_identity(nc, ident[:])
        ds_win = [sbuf("ds_win%d" % t, [P, 2 * S], F32) for t in range(PACK)]
        b_win = [sbuf("b_win%d" % t, [P, 2 * V], F32) for t in range(PACK)]
        for t in range(PACK):
            nc.vector.memset(ds_win[t][:, S:], 0.0)
        for t in range(PACK):
            nc.vector.memset(b_win[t][:, V:], 0.0)
        halves = sbuf("halves", [P, P], F32)
        nc.gpsimd.memset(halves[:], 0.5)

        def scaled(name, source, factor):
            tile = sbuf(name, [P, PACK], F32)
            nc.gpsimd.tensor_scalar(tile[:], source[:], factor, 0.0, ALU.mult, ALU.add)
            return tile

        neg_tau2 = scaled("neg_tau2", tau2_t, -1.0)
        b_gain = scaled("b_gain", gb_t, 1.5)
        neg_tau3 = scaled("neg_tau3", tau3_t, -1.0)

        def gather_packed(name, table, offsets, dtype, tag=None):
            tile = sbuf(name, [P, 16 * offsets.shape[1]], dtype, tag)
            nc.vector.tensor_copy(tile[:], table[:].indirect(offsets[:]))
            return tile

        def deal(grouped, raw, m0):
            width = raw.shape[2] // PACK
            dst = grouped[:].rearrange("p (t m j) -> p m t j", t=PACK, j=PACK)[:, m0 : m0 + width]
            return dst, raw[:].rearrange("p j (m t) -> p m t j", t=PACK)

        def quantise(codes, plane, grouped, c0, c1):
            nc.vector.quantize_mx(
                out=codes[:, c0:c1].bitcast(FP8X4), scales=plane[:, c0:c1], in_=grouped[:, PACK * c0 : PACK * c1]
            )

        def product(acc, codes, plane, t, moving, moving_plane):
            cols = slice(P * t, P * t + P)
            nc.tensor.matmul_mx(
                out=acc,
                lhsT=codes[:, cols].bitcast(FP8X4),
                lhsT_scale=plane[:, cols],
                rhs=moving[:].bitcast(FP8X4),
                rhs_scale=moving_plane[:],
                start=True,
                stop=True,
            )

        two_b = gather_packed("two_b", scales, two_l, U8)
        two_w = gather_packed("two_w", words, two_l, U32)
        offs_b = gather_packed("offs_b", scales, offs_l, U8)

        w2_g = sbuf("w2_g", [P, PACK * H], BF16)
        nc.scalar.copy(*deal(w2_g, w2_raw[0], 0))
        neg_sl = sbuf("neg_sl", [P, PACK], F32)
        nc.scalar.activation(neg_sl[:], sl_t[:], ACT.Copy, scale=-1.0)
        nc.vector.tensor_copy(*deal(w2_g, w2_raw[1], 48))
        sg_bias = sbuf("sg_bias", [P, PACK], F32)
        nc.vector.tensor_tensor(sg_bias[:], neg_sl[:], th_t[:], ALU.mult)
        w2_c0 = sbuf("w2_c0", [P, P], U32)
        w2_s0 = sbuf("w2_s0", [P, P], U8)
        w2_c = sbuf("w2_c", [P, H], U32)
        w2_s = sbuf("w2_s", [P, H], U8)
        quantise(w2_c0, w2_s0, w2_g, 0, P)
        quantise(w2_c, w2_s, w2_g, P, H)

        sg = sbuf("sg", [P, PACK, S], F32)
        for t in range(PACK):
            d_ps = bank("d_ps%d" % t, [P, S], 0)
            if t == 0:
                product(d_ps[:], w2_c0, w2_s0, t, two_w, two_b)
                nc.vector.tensor_copy(ds_win[t][:, :S], d_ps[:])
            else:
                product(d_ps[:], w2_c, w2_s, t, two_w, two_b)
                nc.scalar.copy(ds_win[t][:, :S], d_ps[:])
            nc.scalar.activation(
                sg[:, t, :], ds_win[t][:].indirect(n1_l[:]), ACT.Sigmoid,
                bias=sg_bias[:, t : t + 1], scale=sl_t[:, t : t + 1],
            )

        neg_tau = sbuf("neg_tau", [P, PACK], F32, tag="sg_bias")
        nc.scalar.activation(neg_tau[:], tau_t[:], ACT.Copy, scale=-1.0)
        three_b = gather_packed("three_b", scales, three_l, U8, tag="w2_g")
        three_w = gather_packed("three_w", words, three_l, U32, tag="w2_s0")
        w3_g = sbuf("w3_g", [P, PACK * H], BF16)
        nc.vector.tensor_copy(*deal(w3_g, w3_raw, 0))
        offs_w = gather_packed("offs_w", words, offs_l, U32, tag="w2_c0")
        w3_c = sbuf("w3_c", [P, H], U32)
        w3_s = sbuf("w3_s", [P, H], U8)
        quantise(w3_c, w3_s, w3_g, 0, H)
        b_ps = [bank("b_ps%d" % u, [P, 2, V], 2 + u) for u in range(2)]
        for t in range(PACK):
            product(b_ps[t // 2][:, t % 2, :], w3_c, w3_s, t, three_w, three_b)
        w1_g = sbuf("w1_g", [P, PACK * H], BF16)
        nc.vector.tensor_copy(*deal(w1_g, w1_raw, 0))
        w1_c = sbuf("w1_c", [P, H], U32)
        w1_s = sbuf("w1_s", [P, H], U8)
        extremes = sbuf("extremes", [P, 2, PACK], F32, tag="w1_raw")
        top, low = extremes[:, 0, :], extremes[:, 1, :]
        ea_bias = [sbuf("ea_bias%d" % u, [P, 2], F32) for u in range(2)]
        ea2_bias = [sbuf("ea2_bias%d" % u, [P, 2], F32) for u in range(2)]
        y_ps = [bank("y_ps%d" % t, [P, S], 4 + t) for t in range(PACK)]
        for u in range(2):
            pair = slice(2 * u, 2 * u + 2)
            for e in range(2):
                t = 2 * u + e
                nc.vector.tensor_scalar(
                    b_win[t][:, :V], b_ps[u][:, e, :], 1.0, None, ALU.mult, ALU.max, accum_out=top[:, t : t + 1]
                )
                if t == 0:
                    quantise(w1_c, w1_s, w1_g, 0, H)
                    for r in range(PACK):
                        product(y_ps[r][:], w1_c, w1_s, r, offs_w, offs_b)
            nc.vector.tensor_reduce(low[:, pair], b_ps[u][:], AXIS_X, ALU.min)
            nc.vector.tensor_tensor(ea_bias[u][:], top[:, pair], neg_tau[:, pair], ALU.mult)
            nc.vector.tensor_tensor(ea2_bias[u][:], low[:, pair], tau2_t[:, pair], ALU.mult)
        y_win = [sbuf("y_win%d" % t, [P, S], F32) for t in range(PACK)]

        def y_out(t):
            nc.vector.tensor_scalar(y_win[t][:], y_ps[t][:], ga_t[:, t : t + 1], None, ALU.mult)

        def weave_out(grouped):
            return grouped[:].rearrange("p (c i t) -> p c t i", i=2, t=PACK)

        def weave_in(planes):
            return planes.rearrange("p t (c i) -> p c t i", i=2)

        z_g = [sbuf("z_g%d" % m, [P, PACK * P], BF16) for m in range(4)]
        z_c = [sbuf("z_c%d" % m, [P, P], U32) for m in range(4)]
        z_s = [sbuf("z_s%d" % m, [P, P], U8) for m in range(4)]

        def gate(h, t):
            cols = slice(HALF * h, HALF * h + HALF)
            nc.vector.scalar_tensor_tensor(
                gated[h][:, t, :], y_ps[t][:, cols], ga_t[:, t : t + 1], sg[:, t, cols], ALU.mult, ALU.mult
            )

        def add_picked(m):
            h, e = divmod(m, 2)
            nc.vector.tensor_tensor(
                weave_out(z_g[m]), weave_in(picked[:, h, :, P * e : P * e + P]),
                weave_in(gated[h][:, :, P * e : P * e + P]), ALU.add,
            )

        def quantise_z(m):
            quantise(z_c[m], z_s[m], z_g[m], 0, P)

        ea = sbuf("ea", [P, PACK, V], F32)
        ea2 = sbuf("ea2", [P, PACK, V], F32)
        both = sbuf("both", [P, PACK, V], F32)
        z2 = sbuf("z2", [P, PACK, V], F32)
        for t in range(PACK):
            u, e = divmod(t, 2)
            nc.scalar.activation(
                ea[:, t, :], b_win[t][:].indirect(n3_l[:]), ACT.Exp,
                bias=ea_bias[u][:, e : e + 1], scale=tau_t[:, t : t + 1],
            )
            nc.scalar.activation(
                ea2[:, t, :], b_win[t][:].indirect(n4_l[:]), ACT.Exp,
                bias=ea2_bias[u][:, e : e + 1], scale=neg_tau2[:, t : t + 1],
            )

        for t in range(PACK):
            nc.gpsimd.tensor_tensor(both[:, t, :], ea[:, t, :], ea2[:, t, :], ALU.add)

        def weigh(t):
            nc.vector.scalar_tensor_tensor(
                z2[:, t, :], b_ps[t // 2][:, t % 2, :], b_gain[:, t : t + 1], both[:, t, :], ALU.mult, ALU.mult
            )

        gated = [sbuf("gated0", [P, PACK, HALF], F32, "sg_bias")]
        y_out(0)
        y_out(1)
        gate(0, 0)
        weigh(0)
        y_out(2)
        gate(0, 1)
        weigh(1)
        y_out(3)
        gate(0, 2)
        weigh(2)
        gate(0, 3)
        weigh(3)
        gated.append(sbuf("gated1", [P, PACK, HALF], F32, "ea"))
        picked = sbuf("picked", [P, 2, PACK, HALF], F32, "ea2_bias1")
        for h in range(2):
            for t in range(PACK):
                nc.scalar.activation(
                    picked[:, h, t, :], y_win[t][:].indirect(n2_l[:, 16 * h : 16 * h + 16]), ACT.Copy, scale=-0.5
                )
        z2_g = sbuf("z2_g", [P, PACK * V], BF16)
        z2_c = sbuf("z2_c", [P, V], U32)
        z2_s = sbuf("z2_s", [P, V], U8)
        gate(1, 0)
        nc.vector.tensor_copy(weave_out(z2_g), weave_in(z2[:]))
        add_picked(0)
        quantise(z2_c, z2_s, z2_g, 0, V)
        quantise_z(0)

        top2 = sbuf("top2", [P, 4], F32)
        ea3_bias = sbuf("ea3_bias", [P, 4], F32)

        def scores(m):
            s_ps = bank("s_ps%d" % m, [P, V], m)
            product(s_ps[:], z_c[m], z_s[m], 0, z2_c, z2_s)
            nc.vector.tensor_scalar(
                ds_win[m][:, :V], s_ps[:], 0.0625, None, ALU.mult, ALU.max, accum_out=top2[:, m : m + 1]
            )

        def scores_bias(m):
            nc.vector.tensor_tensor(ea3_bias[:, m : m + 1], top2[:, m : m + 1], neg_tau3[:, m : m + 1], ALU.mult)

        add_picked(1)
        scores(0)
        quantise_z(1)
        scores_bias(0)
        gate(1, 1)
        gate(1, 2)
        scores(1)
        gate(1, 3)
        scores_bias(1)
        add_picked(2)
        add_picked(3)
        quantise_z(2)
        quantise_z(3)
        scores(2)
        scores(3)
        scores_bias(2)
        scores_bias(3)

        sums_ps = [bank("sums_ps%d" % m, [P, 2, P], m + 1) for m in range(2)]
        ea3 = [sbuf("ea3_%d" % m, [P, W], F32) for m in range(4)]
        for m in range(4):
            for g in range(2):
                nc.scalar.activation(
                    ea3[m][:, 512 * g : 512 * g + 512], ds_win[m][:].indirect(n5_l[:, 32 * g : 32 * g + 32]), ACT.Exp,
                    bias=ea3_bias[:, m : m + 1], scale=tau3_t[:, m : m + 1],
                )
                if m < 2:
                    terms = [ea3[m][:, 512 * g + member : 512 * g + 512 : 4] for member in range(4)]
                    if m == 0:
                        terms.append(halves[:])
                    for place, term in enumerate(terms):
                        nc.tensor.matmul(
                            sums_ps[m][:, g, :], term, ident[:],
                            is_transpose=True, start=(place == 0), stop=(place == len(terms) - 1),
                        )

        def turn_back_and_store(m, inverse):
            inverse_ps = bank("inverse_ps%d" % m, [P, V], 4 + m)
            for g in range(2):
                nc.tensor.transpose(inverse_ps[:, P * g : P * g + P], inverse[:, P * g : P * g + P], ident[:])
            result = sbuf("result%d" % m, [P, V], F32)
            nc.vector.scalar_tensor_tensor(result[:], ds_win[m][:, :V], 1.5, inverse_ps[:], ALU.mult, ALU.mult)
            nc.sync.dma_start(out[P * m : P * m + P, :], result[:])

        inverse0 = sbuf("inverse0", [P, V], F32, tag="neg_tau3")
        nc.vector.reciprocal(inverse0[:], sums_ps[0][:].rearrange("p g i -> p (g i)"))
        sums = sbuf("sums", [P, 2, V], F32, tag="top2")
        nc.vector.tensor_reduce(sums[:, 0, :], ea3[2][:].rearrange("p (v d) -> p v d", d=4), AXIS_X, ALU.add)
        turn_back_and_store(0, inverse0)
        nc.vector.tensor_reduce(sums[:, 1, :], ea3[3][:].rearrange("p (v d) -> p v d", d=4), AXIS_X, ALU.add)
        root = sbuf("root", [P, 4, V], F32, tag="ea3_bias")
        once = {}
        for m in (2, 3):
            nc.scalar.activation(root[:, m, :], sums[:, m - 2, :], ACT.Abs_reciprocal_sqrt, bias=0.5)
            once[m] = sbuf("once%d" % m, [P, V], F32)
            nc.vector.scalar_tensor_tensor(once[m][:], ds_win[m][:, :V], 1.5, root[:, m, :], ALU.mult, ALU.mult)
        for m in (2, 3):
            result = sbuf("result%d" % m, [P, V], F32)
            nc.vector.tensor_tensor(result[:], once[m][:], root[:, m, :], ALU.mult)
            nc.sync.dma_start(out[P * m : P * m + P, :], result[:])
        nc.scalar.activation(
            root[:, 1, :], sums_ps[1][:].rearrange("p g i -> p (g i)"), ACT.Abs_reciprocal_sqrt, bias=0.5
        )
        inverse1 = sbuf("inverse1", [P, V], F32)
        nc.scalar.activation(inverse1[:], root[:, 1, :], ACT.Square)
        turn_back_and_store(1, inverse1)
